import numpy as np
import ml_dtypes


def mxq(x, axis, fmt="e4m3"):
    dtype, down = {"e4m3": (ml_dtypes.float8_e4m3fn, 7), "e5m2": (ml_dtypes.float8_e5m2, 14)}[fmt]
    v = np.moveaxis(np.asarray(x, np.float32).astype(ml_dtypes.bfloat16).astype(np.float64), axis, -1)
    blocks = v.reshape(v.shape[:-1] + (-1, 32))
    amax = np.abs(blocks).max(-1, keepdims=True)
    byte = np.maximum(np.where(amax > 0, np.frexp(amax)[1] - 1 + 127, 0) - down, 1)
    scale = np.exp2(byte - 127.0)
    codes = (blocks / scale).astype(np.float32).astype(dtype).astype(np.float64)
    return np.moveaxis((codes * scale).reshape(v.shape), -1, axis)


WIDE = False


def mx_kscale(k):
    if not WIDE:
        return np.ones(k)
    levels = np.array([30, -30])
    if k % 512:
        return np.exp2(np.random.permutation(np.resize(levels, k // 32))).repeat(32)
    a = np.empty((k // 512, 16))
    for p in range(k // 512):
        a[p, :8] = np.random.permutation(np.resize(levels, 8))
        for g in range(8):
            far = levels[np.abs(levels - a[p, g]) >= 10]
            a[p, g + 8] = far[np.random.randint(len(far))]
    return np.exp2(a.ravel()).repeat(32)


def f64(x):
    return np.asarray(x).astype(np.float64)


def striped(idx):
    return np.tile(np.asarray(idx).reshape(-1, 16).T, (8, 1)).astype(np.uint16)


def unstriped(offs):
    return offs[:16].T.reshape(-1).astype(np.int64)


E2M1 = np.array([0.0, 0.5, 1.0, 1.5, 2.0, 3.0, 4.0, 6.0, -0.0, -0.5, -1.0, -1.5, -2.0, -3.0, -4.0, -6.0])


def pack_weight(w, fmt):
    k, n = w.shape
    w = f64(np.asarray(w, np.float32).astype(ml_dtypes.bfloat16)).reshape(k // 32, 32, n)
    amax = np.abs(w).max(1)
    if fmt in ("e4m3", "e5m2"):
        byte = np.frexp(amax)[1] - 1 + 127 - (7 if fmt == "e4m3" else 14)
    else:
        mant, ex = np.frexp(amax / 6.0)
        byte = np.where(mant > 0.5, ex, ex - 1) + 127
    byte = np.clip(np.where(amax > 0, byte, 1), 1, 254)
    scaled = (w * np.exp2(127.0 - byte)[:, None, :]).reshape(k, n).astype(np.float32)
    by_word = np.ascontiguousarray(scaled.reshape(k // 512, 128, 4, n).transpose(0, 1, 3, 2))
    if fmt in ("e4m3", "e5m2"):
        words = by_word.astype(ml_dtypes.float8_e4m3fn if fmt == "e4m3" else ml_dtypes.float8_e5m2).view(np.uint8)
    else:
        c = by_word.astype(ml_dtypes.float4_e2m1fn).view(np.uint8) & 0xF
        words = (c[..., 0::2] | (c[..., 1::2] << 4)).reshape(k // 512, 128, 2 * n)
    return np.ascontiguousarray(words), np.ascontiguousarray(byte.astype(np.uint8).reshape(k // 512, 16, n))


def unpack_weight(words, scales, fmt):
    g, _, n = scales.shape
    words = np.ascontiguousarray(words).reshape(g, 128, n, -1)
    if fmt in ("e4m3", "e5m2"):
        vals = words.view(ml_dtypes.float8_e4m3fn if fmt == "e4m3" else ml_dtypes.float8_e5m2).astype(np.float64)
    else:
        nib = np.empty((g, 128, n, 4), np.uint8)
        nib[..., 0::2] = words & 0xF
        nib[..., 1::2] = words >> 4
        vals = E2M1[nib]
    vals = vals * np.repeat(np.exp2(scales.astype(np.float64) - 127.0), 8, axis=1)[..., None]
    return vals.transpose(0, 1, 3, 2).reshape(g * 512, n)


def bf(x):
    return np.asarray(x, np.float32).astype(ml_dtypes.bfloat16)


def planes(Y):
    r, m = Y.shape
    b = f64(bf(Y)).reshape(r // 32, 32, m)
    amax = np.abs(b).max(1)
    byte = np.clip(np.where(amax > 0, np.frexp(amax)[1] - 1 + 127 - 7, 1), 1, 254)
    codes = (b * np.exp2(127.0 - byte)[:, None, :]).reshape(r, m).astype(np.float32).astype(ml_dtypes.float8_e4m3fn).view(np.uint8)
    words = codes.reshape(r // 512, 128, 4, m).transpose(0, 1, 3, 2)
    return np.ascontiguousarray(words), np.ascontiguousarray(byte.astype(np.uint8).reshape(r // 512, 16, m))


K, T, J, R, V, N = 512, 1024, 256, 512, 512, 512


def setup_inputs():
    n = np.random.standard_normal
    idx = np.random.permutation(T)[:J]
    idx2 = np.random.permutation(V)[:J]
    fk = mx_kscale(K)
    fr = mx_kscale(R)
    wp = pack_weight(n((K, R)) * 1 / np.sqrt(K) * fk[:, None] * fr, "e2m1")
    wbp = pack_weight(n((R, N)) * 1 / np.sqrt(R) / fr[:, None], "e5m2")
    return {
        "xf": (n((K, T))).astype(np.float32),
        "ow": (n((K, J)) * 0.7).astype(np.float32),
        "fk": (np.random.uniform(0.5, 2.0, (K, 1)) / fk[:, None]).astype(np.float32),
        "w_words": wp[0],
        "w_scales": wp[1],
        "tb": (n((R, V)) * 0.7).astype(np.float32),
        "wb_words": wbp[0],
        "wb_scales": wbp[1],
        "rs": (n((N, J))).astype(np.float32),
        "gm": (np.random.uniform(0.5, 2.0, (N, 1))).astype(np.float32),
        "offs": striped(idx),
        "offs2": striped(idx2),
    }


def reference(xf, ow, fk, w_words, w_scales, tb, wb_words, wb_scales, rs, gm, offs, offs2):
    idx = unstriped(offs)
    idx2 = unstriped(offs2)
    wu = unpack_weight(w_words, w_scales, "e2m1")
    wbu = unpack_weight(wb_words, wb_scales, "e5m2")
    u = (f64(xf)[:, idx] - f64(ow)) * f64(fk)
    uq = mxq(u, 0, "e4m3")
    a = wu.T @ uq
    hid = np.maximum(a, 0.0) * f64(tb)[:, idx2]
    hidq = mxq(hid, 0, "e5m2")
    p = wbu.T @ hidq
    y = f64(gm) * p + f64(rs)
    words, scales = planes(y)
    return y, words, scales

@@ -1,0 +1,221 @@
+from contextlib import ExitStack
+
+import concourse.mybir as mybir
+
+K, T, J, R, V, N = 512, 1024, 256, 512, 512, 512
+FLOPS = 2 * K * R * J + 2 * R * N * J
+
+F32 = mybir.dt.float32
+BF16 = mybir.dt.bfloat16
+I32 = mybir.dt.int32
+U32 = mybir.dt.uint32
+U16 = mybir.dt.uint16
+U8 = mybir.dt.uint8
+E4M3 = mybir.dt.float8_e4m3fn_x4
+E5M2 = mybir.dt.float8_e5m2_x4
+E2M1 = mybir.dt.float4_e2m1fn_x4
+ALU = mybir.AluOpType
+COPY = mybir.ActivationFunctionType.Copy
+
+P = 128
+PACK = 4
+HALF = J // 2
+HALVES = (slice(0, HALF), slice(HALF, J))
+LIST_HALVES = (slice(0, HALF // 16), slice(HALF // 16, J // 16))
+
+
+def load_scale_rows(queue, plane, scales):
+    for q in range(4):
+        queue.dma_start(out=plane[32 * q : 32 * q + 4, :].bitcast(I32), in_=scales[0, 4 * q : 4 * q + 4, :].bitcast(I32))
+
+
+def deal_scales(nc, dealt, plane):
+    nc.vector.tensor_copy(
+        out=dealt.rearrange("p (t c i) -> p c t i", t=PACK, i=16),
+        in_=plane.rearrange("p (c i t) -> p c t i", t=PACK, i=16),
+    )
+
+
+def tile_list_offsetpicks_timestable_residual_pl_kernel(
+    tc, xf, ow, fk, w_words, w_scales, tb, wb_words, wb_scales, rs, gm, offs, offs2, out_0, out_1, out_2
+):
+    nc = tc.nc
+    with ExitStack() as ctx:
+        keep = ctx.enter_context(tc.tile_pool(name="keep", bufs=1))
+        psum = ctx.enter_context(tc.psum_pool(name="psum", bufs=1))
+
+        def by_slot(x):
+            return x.rearrange("(p t) c -> p t c", t=PACK)
+
+        x_list = keep.tile([P, J // 16], U16, name="x_list")
+        tb_list = keep.tile([P, J // 16], U16, name="tb_list")
+        xf_sb = [keep.tile([P, T], F32, name="xf%d" % t) for t in range(PACK)]
+        tb_pair = keep.tile([P, 2, V], F32, name="tb_pair")
+        tb_rest = [keep.tile([P, V], F32, name="tb%d" % t) for t in range(2, PACK)]
+        tb_sb = [tb_pair[:, 0, :], tb_pair[:, 1, :], tb_rest[0][:], tb_rest[1][:]]
+        ow_sb = keep.tile([P, PACK, J], F32, name="ow_sb")
+        rs_sb = keep.tile([P, PACK, J], F32, name="rs_sb")
+        fk_sb = keep.tile([P, PACK], F32, name="fk_sb")
+        gm_sb = keep.tile([P, PACK], F32, name="gm_sb")
+        w_raw = keep.tile([P, 2 * R], U8, name="w_raw")
+        wb_raw = keep.tile([P, N], U32, name="wb_raw")
+        ws_raw = keep.tile([P, R], U8, name="ws_raw")
+        wbs_raw = keep.tile([P, N], U8, name="wbs_raw")
+        w_d = keep.tile([P, 2 * R], U8, name="w_d", align_bytes=64)
+        wb_d = keep.tile([P, N], U32, name="wb_d", align_bytes=64)
+        ws_d = keep.tile([P, R], U8, name="ws_d", align_bytes=64)
+        wbs_d = keep.tile([P, N], U8, name="wbs_d", align_bytes=64)
+
+        nc.vector.memset(ws_raw[:].bitcast(I32), 0)
+        nc.vector.memset(wbs_raw[:].bitcast(I32), 0)
+
+        nc.sync.dma_start(out=xf_sb[0][:], in_=by_slot(xf)[:, 0, :])
+        nc.scalar.dma_start(out=w_raw[:].bitcast(I32), in_=w_words[0].bitcast(I32))
+        nc.sync.dma_start(x_list[:], offs)
+        nc.gpsimd.dma_start(out=fk_sb[:], in_=fk.rearrange("(p t) o -> p (t o)", t=PACK))
+        nc.sync.dma_start(out=ow_sb[:], in_=by_slot(ow))
+        load_scale_rows(nc.scalar, ws_raw, w_scales)
+        for t in range(1, PACK):
+            nc.sync.dma_start(out=xf_sb[t][:], in_=by_slot(xf)[:, t, :])
+        load_scale_rows(nc.scalar, wbs_raw, wb_scales)
+        nc.gpsimd.dma_start(out=gm_sb[:], in_=gm.rearrange("(p t) o -> p (t o)", t=PACK))
+        nc.sync.dma_start(tb_list[:], offs2)
+        nc.sync.dma_start(out=tb_pair[:], in_=by_slot(tb)[:, 0:2, :])
+        for t in range(2, PACK):
+            nc.sync.dma_start(out=tb_sb[t], in_=by_slot(tb)[:, t, :])
+        nc.sync.dma_start(
+            out=wb_raw[:].bitcast(I32), in_=wb_words[0].rearrange("p c r -> p (c r)").bitcast(I32)
+        )
+        nc.sync.dma_start(out=rs_sb[:], in_=by_slot(rs))
+
+        nc.vector.tensor_copy(
+            out=w_d[:].rearrange("p (t c i b) -> p c t i b", t=PACK, i=8, b=2),
+            in_=w_raw[:].rearrange("p (c i t b) -> p c t i b", t=PACK, i=8, b=2),
+        )
+        deal_scales(nc, ws_d[:], ws_raw[:])
+
+        diff = [keep.tile([P, J], F32, name="diff%d" % t) for t in range(PACK)]
+        u_bf = keep.tile([P, J, PACK], BF16, name="u_bf", align_bytes=64)
+        u_codes = keep.tile([P, J], U32, name="u_codes", align_bytes=64)
+        u_scales = keep.tile([P, J], U8, name="u_scales", align_bytes=64)
+        last = PACK - 1
+        for t in range(last):
+            nc.vector.tensor_tensor(diff[t][:], xf_sb[t][:].indirect(x_list[:]), ow_sb[:, t, :], ALU.subtract)
+            if t < 2:
+                nc.scalar.activation(out=u_bf[:, :, t], in_=diff[t][:], func=COPY, scale=fk_sb[:, t : t + 1])
+            else:
+                nc.vector.tensor_scalar(
+                    out=u_bf[:, :, t], in0=diff[t][:], scalar1=fk_sb[:, t : t + 1], scalar2=None, op0=ALU.mult
+                )
+            if t == 0:
+                deal_scales(nc, wbs_d[:], wbs_raw[:])
+        for h in range(2):
+            nc.vector.tensor_tensor(
+                diff[last][:, HALVES[h]],
+                xf_sb[last][:].indirect(x_list[:, LIST_HALVES[h]]),
+                ow_sb[:, last, HALVES[h]],
+                ALU.subtract,
+            )
+        for h in range(2):
+            nc.vector.tensor_scalar(
+                out=u_bf[:, HALVES[h], last],
+                in0=diff[last][:, HALVES[h]],
+                scalar1=fk_sb[:, last : last + 1],
+                scalar2=None,
+                op0=ALU.mult,
+            )
+        a_ps = [psum.tile([P, PACK, HALF], F32, name="a_ps%d" % h) for h in range(2)]
+        for h in range(2):
+            nc.vector.quantize_mx(
+                out=u_codes[:, HALVES[h]].bitcast(E4M3),
+                scales=u_scales[:, HALVES[h]],
+                in_=u_bf[:, HALVES[h], :].rearrange("p j t -> p (j t)"),
+            )
+            for t in range(PACK):
+                nc.tensor.matmul_mx(
+                    out=a_ps[h][:, t, :],
+                    lhsT=w_d[:, 2 * P * t : 2 * P * (t + 1)].bitcast(E2M1),
+                    lhsT_scale=ws_d[:, P * t : P * (t + 1)],
+                    rhs=u_codes[:, HALVES[h]].bitcast(E4M3),
+                    rhs_scale=u_scales[:, HALVES[h]],
+                    start=True,
+                    stop=True,
+                )
+
+        tb_g = [keep.tile([P, PACK, HALF], F32, name="tb_g%d" % h) for h in range(2)]
+        for t in range(PACK):
+            for h in range(2):
+                nc.scalar.activation(
+                    out=tb_g[h][:, t, :], in_=tb_sb[t].indirect(tb_list[:, LIST_HALVES[h]]), func=COPY
+                )
+
+        hid_bf = [keep.tile([P, HALF, PACK], BF16, name="hid_bf%d" % h, align_bytes=64) for h in range(2)]
+        hid_codes = [keep.tile([P, HALF], U32, name="hid_codes%d" % h, align_bytes=64) for h in range(2)]
+        hid_scales = [keep.tile([P, HALF], U8, name="hid_scales%d" % h, align_bytes=64) for h in range(2)]
+        p_ps = [psum.tile([P, PACK, HALF], F32, name="p_ps%d" % h) for h in range(2)]
+        for h in range(2):
+            nc.vector.scalar_tensor_tensor(
+                out=hid_bf[h][:],
+                in0=a_ps[h][:].rearrange("p t j -> p j t"),
+                scalar=0.0,
+                in1=tb_g[h][:].rearrange("p t j -> p j t"),
+                op0=ALU.max,
+                op1=ALU.mult,
+            )
+            if h == 0:
+                nc.vector.tensor_copy(
+                    out=wb_d[:].rearrange("p (t c i) -> p c t i", t=PACK, i=4),
+                    in_=wb_raw[:].rearrange("p (c i t) -> p c t i", t=PACK, i=4),
+                )
+            nc.vector.quantize_mx(
+                out=hid_codes[h][:].bitcast(E5M2),
+                scales=hid_scales[h][:],
+                in_=hid_bf[h][:].rearrange("p j t -> p (j t)"),
+            )
+            for t in range(PACK):
+                nc.tensor.matmul_mx(
+                    out=p_ps[h][:, t, :],
+                    lhsT=wb_d[:, P * t : P * (t + 1)].bitcast(E5M2),
+                    lhsT_scale=wbs_d[:, P * t : P * (t + 1)],
+                    rhs=hid_codes[h][:].bitcast(E5M2),
+                    rhs_scale=hid_scales[h][:],
+                    start=True,
+                    stop=True,
+                )
+
+        y = [keep.tile([P, PACK, HALF], F32, name="y%d" % h) for h in range(2)]
+        y_bf = [keep.tile([P, HALF, PACK], BF16, name="y_bf%d" % h, align_bytes=64) for h in range(2)]
+        y_codes = [keep.tile([P, HALF], U32, name="y_codes%d" % h, align_bytes=64) for h in range(2)]
+        y_scales = keep.tile([P, J], U8, name="y_scales", align_bytes=64)
+        for h in range(2):
+            for t in range(PACK):
+                nc.vector.scalar_tensor_tensor(
+                    out=y[h][:, t, :],
+                    in0=p_ps[h][:, t, :],
+                    scalar=gm_sb[:, t : t + 1],
+                    in1=rs_sb[:, t, HALVES[h]],
+                    op0=ALU.mult,
+                    op1=ALU.add,
+                )
+            nc.sync.dma_start(out=by_slot(out_0)[:, :, HALVES[h]], in_=y[h][:])
+        for h in range(2):
+            woven = y_bf[h][:].rearrange("p (c i) t -> p c t i", i=4)
+            source = y[h][:].rearrange("p t (c i) -> p c t i", i=4)
+            if h == 0:
+                nc.scalar.copy(out=woven, in_=source)
+            else:
+                nc.vector.tensor_copy(out=woven, in_=source)
+            nc.vector.quantize_mx(
+                out=y_codes[h][:].bitcast(E4M3),
+                scales=y_scales[:, HALVES[h]],
+                in_=y_bf[h][:].rearrange("p j t -> p (j t)"),
+            )
+            nc.scalar.dma_start(
+                out=out_1[0, :, HALVES[h], :].rearrange("p j r -> p (j r)").bitcast(I32),
+                in_=y_codes[h][:].bitcast(I32),
+            )
+        for q in range(4):
+            queue = nc.sync if q % 2 == 0 else nc.scalar
+            queue.dma_start(
+                out=out_2[0, 4 * q : 4 * q + 4, :].bitcast(I32), in_=y_scales[32 * q : 32 * q + 4, :].bitcast(I32)
+            )

@@ -53,7 +53,7 @@ def tile_list_offsetpicks_timestable_residual_pl_kernel(
         tb_pair = keep.tile([P, 2, V], F32, name="tb_pair")
         tb_rest = [keep.tile([P, V], F32, name="tb%d" % t) for t in range(2, PACK)]
         tb_sb = [tb_pair[:, 0, :], tb_pair[:, 1, :], tb_rest[0][:], tb_rest[1][:]]
-        ow_sb = keep.tile([P, PACK, J], F32, name="ow_sb")
+        ow_sb = keep.tile([P, PACK, J], F32, name="ow_sb", tag="reuse_ow", align_bytes=64)
         rs_sb = keep.tile([P, PACK, J], F32, name="rs_sb")
         fk_sb = keep.tile([P, PACK], F32, name="fk_sb")
         gm_sb = keep.tile([P, PACK], F32, name="gm_sb")
@@ -62,24 +62,23 @@ def tile_list_offsetpicks_timestable_residual_pl_kernel(
         ws_raw = keep.tile([P, R], U8, name="ws_raw")
         wbs_raw = keep.tile([P, N], U8, name="wbs_raw")
         w_d = keep.tile([P, 2 * R], U8, name="w_d", align_bytes=64)
-        wb_d = keep.tile([P, N], U32, name="wb_d", align_bytes=64)
         ws_d = keep.tile([P, R], U8, name="ws_d", align_bytes=64)
-        wbs_d = keep.tile([P, N], U8, name="wbs_d", align_bytes=64)
 
         nc.vector.memset(ws_raw[:].bitcast(I32), 0)
         nc.vector.memset(wbs_raw[:].bitcast(I32), 0)
 
-        nc.sync.dma_start(out=xf_sb[0][:], in_=by_slot(xf)[:, 0, :])
-        nc.scalar.dma_start(out=w_raw[:].bitcast(I32), in_=w_words[0].bitcast(I32))
-        nc.sync.dma_start(x_list[:], offs)
         nc.gpsimd.dma_start(out=fk_sb[:], in_=fk.rearrange("(p t) o -> p (t o)", t=PACK))
-        nc.sync.dma_start(out=ow_sb[:], in_=by_slot(ow))
-        load_scale_rows(nc.scalar, ws_raw, w_scales)
-        for t in range(1, PACK):
-            nc.sync.dma_start(out=xf_sb[t][:], in_=by_slot(xf)[:, t, :])
-        load_scale_rows(nc.scalar, wbs_raw, wb_scales)
         nc.gpsimd.dma_start(out=gm_sb[:], in_=gm.rearrange("(p t) o -> p (t o)", t=PACK))
+        nc.sync.dma_start(out=xf_sb[0][:], in_=by_slot(xf)[:, 0, :])
+        nc.sync.dma_start(x_list[:], offs)
+        nc.sync.dma_start(out=ow_sb[:], in_=by_slot(ow))
+        load_scale_rows(nc.sync, ws_raw, w_scales)
+        nc.sync.dma_start(out=xf_sb[1][:], in_=by_slot(xf)[:, 1, :])
+        nc.sync.dma_start(out=w_raw[:].bitcast(I32), in_=w_words[0].bitcast(I32))
+        nc.sync.dma_start(out=xf_sb[2][:], in_=by_slot(xf)[:, 2, :])
         nc.sync.dma_start(tb_list[:], offs2)
+        nc.sync.dma_start(out=xf_sb[3][:], in_=by_slot(xf)[:, 3, :])
+        load_scale_rows(nc.sync, wbs_raw, wb_scales)
         nc.sync.dma_start(out=tb_pair[:], in_=by_slot(tb)[:, 0:2, :])
         for t in range(2, PACK):
             nc.sync.dma_start(out=tb_sb[t], in_=by_slot(tb)[:, t, :])
@@ -88,27 +87,22 @@ def tile_list_offsetpicks_timestable_residual_pl_kernel(
         )
         nc.sync.dma_start(out=rs_sb[:], in_=by_slot(rs))
 
-        nc.vector.tensor_copy(
-            out=w_d[:].rearrange("p (t c i b) -> p c t i b", t=PACK, i=8, b=2),
-            in_=w_raw[:].rearrange("p (c i t b) -> p c t i b", t=PACK, i=8, b=2),
-        )
         deal_scales(nc, ws_d[:], ws_raw[:])
 
-        diff = [keep.tile([P, J], F32, name="diff%d" % t) for t in range(PACK)]
-        u_bf = keep.tile([P, J, PACK], BF16, name="u_bf", align_bytes=64)
+        diff_pair = [keep.tile([P, 2, J], F32, name="diff%d" % i, tag="reuse%d" % i, align_bytes=64) for i in range(2)]
+        diff = [diff_pair[t // 2][:, t % 2, :] for t in range(PACK)]
+        u_bf = keep.tile([P, J, PACK], BF16, name="u_bf", tag="reuse_u", align_bytes=64)
         u_codes = keep.tile([P, J], U32, name="u_codes", align_bytes=64)
         u_scales = keep.tile([P, J], U8, name="u_scales", align_bytes=64)
         last = PACK - 1
         for t in range(last):
-            nc.vector.tensor_tensor(diff[t][:], xf_sb[t][:].indirect(x_list[:]), ow_sb[:, t, :], ALU.subtract)
-            if t < 2:
-                nc.scalar.activation(out=u_bf[:, :, t], in_=diff[t][:], func=COPY, scale=fk_sb[:, t : t + 1])
-            else:
-                nc.vector.tensor_scalar(
-                    out=u_bf[:, :, t], in0=diff[t][:], scalar1=fk_sb[:, t : t + 1], scalar2=None, op0=ALU.mult
+            nc.vector.tensor_tensor(diff[t], xf_sb[t][:].indirect(x_list[:]), ow_sb[:, t, :], ALU.subtract)
+            nc.scalar.activation(out=u_bf[:, :, t], in_=diff[t], func=COPY, scale=fk_sb[:, t : t + 1])
+            if t == 1:
+                nc.vector.tensor_copy(
+                    out=w_d[:].bitcast(U16).rearrange("p (t c i) -> p c t i", t=PACK, i=8),
+                    in_=w_raw[:].bitcast(U16).rearrange("p (c i t) -> p c t i", t=PACK, i=8),
                 )
-            if t == 0:
-                deal_scales(nc, wbs_d[:], wbs_raw[:])
         for h in range(2):
             nc.vector.tensor_tensor(
                 diff[last][:, HALVES[h]],
@@ -116,14 +110,14 @@ def tile_list_offsetpicks_timestable_residual_pl_kernel(
                 ow_sb[:, last, HALVES[h]],
                 ALU.subtract,
             )
-        for h in range(2):
-            nc.vector.tensor_scalar(
+            nc.scalar.activation(
                 out=u_bf[:, HALVES[h], last],
-                in0=diff[last][:, HALVES[h]],
-                scalar1=fk_sb[:, last : last + 1],
-                scalar2=None,
-                op0=ALU.mult,
+                in_=diff[last][:, HALVES[h]],
+                func=COPY,
+                scale=fk_sb[:, last : last + 1],
             )
+        wbs_d = keep.tile([P, N], U8, name="wbs_d", tag="reuse_ow", align_bytes=64)
+        deal_scales(nc, wbs_d[:], wbs_raw[:])
         a_ps = [psum.tile([P, PACK, HALF], F32, name="a_ps%d" % h) for h in range(2)]
         for h in range(2):
             nc.vector.quantize_mx(
@@ -142,20 +136,25 @@ def tile_list_offsetpicks_timestable_residual_pl_kernel(
                     stop=True,
                 )
 
-        tb_g = [keep.tile([P, PACK, HALF], F32, name="tb_g%d" % h) for h in range(2)]
-        for t in range(PACK):
-            for h in range(2):
-                nc.scalar.activation(
-                    out=tb_g[h][:, t, :], in_=tb_sb[t].indirect(tb_list[:, LIST_HALVES[h]]), func=COPY
-                )
+        tb_g = [
+            keep.tile([P, PACK, HALF], F32, name="tb_g%d" % h, tag=("reuse1", "reuse_u")[h], align_bytes=64)
+            for h in range(2)
+        ]
+        for h in range(2):
+            for t in range(PACK):
+                picked = tb_sb[t].indirect(tb_list[:, LIST_HALVES[h]])
+                if h == 0 and t >= 2:
+                    nc.vector.tensor_copy(out=tb_g[h][:, t, :], in_=picked)
+                else:
+                    nc.scalar.activation(out=tb_g[h][:, t, :], in_=picked, func=COPY)
 
-        hid_bf = [keep.tile([P, HALF, PACK], BF16, name="hid_bf%d" % h, align_bytes=64) for h in range(2)]
         hid_codes = [keep.tile([P, HALF], U32, name="hid_codes%d" % h, align_bytes=64) for h in range(2)]
         hid_scales = [keep.tile([P, HALF], U8, name="hid_scales%d" % h, align_bytes=64) for h in range(2)]
         p_ps = [psum.tile([P, PACK, HALF], F32, name="p_ps%d" % h) for h in range(2)]
         for h in range(2):
+            hid_bf = keep.tile([P, HALF, PACK], BF16, name="hid_bf%d" % h, tag=("hid_bf", "reuse_hid")[h], align_bytes=64)
             nc.vector.scalar_tensor_tensor(
-                out=hid_bf[h][:],
+                out=hid_bf[:],
                 in0=a_ps[h][:].rearrange("p t j -> p j t"),
                 scalar=0.0,
                 in1=tb_g[h][:].rearrange("p t j -> p j t"),
@@ -163,6 +162,7 @@ def tile_list_offsetpicks_timestable_residual_pl_kernel(
                 op1=ALU.mult,
             )
             if h == 0:
+                wb_d = keep.tile([P, N], U32, name="wb_d", align_bytes=64)
                 nc.vector.tensor_copy(
                     out=wb_d[:].rearrange("p (t c i) -> p c t i", t=PACK, i=4),
                     in_=wb_raw[:].rearrange("p (c i t) -> p c t i", t=PACK, i=4),
@@ -170,7 +170,7 @@ def tile_list_offsetpicks_timestable_residual_pl_kernel(
             nc.vector.quantize_mx(
                 out=hid_codes[h][:].bitcast(E5M2),
                 scales=hid_scales[h][:],
-                in_=hid_bf[h][:].rearrange("p j t -> p (j t)"),
+                in_=hid_bf[:].rearrange("p j t -> p (j t)"),
             )
             for t in range(PACK):
                 nc.tensor.matmul_mx(
@@ -183,7 +183,9 @@ def tile_list_offsetpicks_timestable_residual_pl_kernel(
                     stop=True,
                 )
 
-        y = [keep.tile([P, PACK, HALF], F32, name="y%d" % h) for h in range(2)]
+        y = [
+            keep.tile([P, PACK, HALF], F32, name="y%d" % h, tag=("reuse_hid", "y1")[h], align_bytes=64) for h in range(2)
+        ]
         y_bf = [keep.tile([P, HALF, PACK], BF16, name="y_bf%d" % h, align_bytes=64) for h in range(2)]
         y_codes = [keep.tile([P, HALF], U32, name="y_codes%d" % h, align_bytes=64) for h in range(2)]
         y_scales = keep.tile([P, J], U8, name="y_scales", align_bytes=64)

@@ -24,8 +24,8 @@ HALVES = (slice(0, HALF), slice(HALF, J))
 LIST_HALVES = (slice(0, HALF // 16), slice(HALF // 16, J // 16))
 
 
-def load_scale_rows(queue, plane, scales):
-    for q in range(4):
+def load_scale_rows(queue, plane, scales, quadrants):
+    for q in quadrants:
         queue.dma_start(out=plane[32 * q : 32 * q + 4, :].bitcast(I32), in_=scales[0, 4 * q : 4 * q + 4, :].bitcast(I32))
 
 
@@ -53,7 +53,7 @@ def tile_list_offsetpicks_timestable_residual_pl_kernel(
         tb_pair = keep.tile([P, 2, V], F32, name="tb_pair")
         tb_rest = [keep.tile([P, V], F32, name="tb%d" % t) for t in range(2, PACK)]
         tb_sb = [tb_pair[:, 0, :], tb_pair[:, 1, :], tb_rest[0][:], tb_rest[1][:]]
-        ow_sb = keep.tile([P, PACK, J], F32, name="ow_sb", tag="reuse_ow", align_bytes=64)
+        ow_sb = keep.tile([P, PACK, J], F32, name="ow_sb")
         rs_sb = keep.tile([P, PACK, J], F32, name="rs_sb")
         fk_sb = keep.tile([P, PACK], F32, name="fk_sb")
         gm_sb = keep.tile([P, PACK], F32, name="gm_sb")
@@ -61,33 +61,34 @@ def tile_list_offsetpicks_timestable_residual_pl_kernel(
         wb_raw = keep.tile([P, N], U32, name="wb_raw")
         ws_raw = keep.tile([P, R], U8, name="ws_raw")
         wbs_raw = keep.tile([P, N], U8, name="wbs_raw")
-        w_d = keep.tile([P, 2 * R], U8, name="w_d", align_bytes=64)
+        w_d = keep.tile([P, 2 * R], U8, name="w_d", tag="reuse_w", align_bytes=64)
         ws_d = keep.tile([P, R], U8, name="ws_d", align_bytes=64)
 
         nc.vector.memset(ws_raw[:].bitcast(I32), 0)
         nc.vector.memset(wbs_raw[:].bitcast(I32), 0)
 
-        nc.gpsimd.dma_start(out=fk_sb[:], in_=fk.rearrange("(p t) o -> p (t o)", t=PACK))
-        nc.gpsimd.dma_start(out=gm_sb[:], in_=gm.rearrange("(p t) o -> p (t o)", t=PACK))
         nc.sync.dma_start(out=xf_sb[0][:], in_=by_slot(xf)[:, 0, :])
         nc.sync.dma_start(x_list[:], offs)
+        nc.sync.dma_start(out=fk_sb[:], in_=fk.rearrange("(p t) o -> p (t o)", t=PACK))
         nc.sync.dma_start(out=ow_sb[:], in_=by_slot(ow))
-        load_scale_rows(nc.sync, ws_raw, w_scales)
+        load_scale_rows(nc.sync, ws_raw, w_scales, (0, 1, 2))
         nc.sync.dma_start(out=xf_sb[1][:], in_=by_slot(xf)[:, 1, :])
+        load_scale_rows(nc.sync, ws_raw, w_scales, (3,))
         nc.sync.dma_start(out=w_raw[:].bitcast(I32), in_=w_words[0].bitcast(I32))
         nc.sync.dma_start(out=xf_sb[2][:], in_=by_slot(xf)[:, 2, :])
         nc.sync.dma_start(tb_list[:], offs2)
+        load_scale_rows(nc.sync, wbs_raw, wb_scales, (0, 1))
         nc.sync.dma_start(out=xf_sb[3][:], in_=by_slot(xf)[:, 3, :])
-        load_scale_rows(nc.sync, wbs_raw, wb_scales)
+        load_scale_rows(nc.sync, wbs_raw, wb_scales, (2, 3))
         nc.sync.dma_start(out=tb_pair[:], in_=by_slot(tb)[:, 0:2, :])
         for t in range(2, PACK):
             nc.sync.dma_start(out=tb_sb[t], in_=by_slot(tb)[:, t, :])
         nc.sync.dma_start(
             out=wb_raw[:].bitcast(I32), in_=wb_words[0].rearrange("p c r -> p (c r)").bitcast(I32)
         )
+        nc.sync.dma_start(out=gm_sb[:], in_=gm.rearrange("(p t) o -> p (t o)", t=PACK))
         nc.sync.dma_start(out=rs_sb[:], in_=by_slot(rs))
 
-        deal_scales(nc, ws_d[:], ws_raw[:])
 
         diff_pair = [keep.tile([P, 2, J], F32, name="diff%d" % i, tag="reuse%d" % i, align_bytes=64) for i in range(2)]
         diff = [diff_pair[t // 2][:, t % 2, :] for t in range(PACK)]
@@ -103,6 +104,7 @@ def tile_list_offsetpicks_timestable_residual_pl_kernel(
                     out=w_d[:].bitcast(U16).rearrange("p (t c i) -> p c t i", t=PACK, i=8),
                     in_=w_raw[:].bitcast(U16).rearrange("p (c i t) -> p c t i", t=PACK, i=8),
                 )
+                deal_scales(nc, ws_d[:], ws_raw[:])
         for h in range(2):
             nc.vector.tensor_tensor(
                 diff[last][:, HALVES[h]],
@@ -116,7 +118,7 @@ def tile_list_offsetpicks_timestable_residual_pl_kernel(
                 func=COPY,
                 scale=fk_sb[:, last : last + 1],
             )
-        wbs_d = keep.tile([P, N], U8, name="wbs_d", tag="reuse_ow", align_bytes=64)
+        wbs_d = keep.tile([P, N], U8, name="wbs_d", align_bytes=64)
         deal_scales(nc, wbs_d[:], wbs_raw[:])
         a_ps = [psum.tile([P, PACK, HALF], F32, name="a_ps%d" % h) for h in range(2)]
         for h in range(2):
@@ -152,7 +154,7 @@ def tile_list_offsetpicks_timestable_residual_pl_kernel(
         hid_scales = [keep.tile([P, HALF], U8, name="hid_scales%d" % h, align_bytes=64) for h in range(2)]
         p_ps = [psum.tile([P, PACK, HALF], F32, name="p_ps%d" % h) for h in range(2)]
         for h in range(2):
-            hid_bf = keep.tile([P, HALF, PACK], BF16, name="hid_bf%d" % h, tag=("hid_bf", "reuse_hid")[h], align_bytes=64)
+            hid_bf = keep.tile([P, HALF, PACK], BF16, name="hid_bf%d" % h, align_bytes=64)
             nc.vector.scalar_tensor_tensor(
                 out=hid_bf[:],
                 in0=a_ps[h][:].rearrange("p t j -> p j t"),
@@ -162,7 +164,7 @@ def tile_list_offsetpicks_timestable_residual_pl_kernel(
                 op1=ALU.mult,
             )
             if h == 0:
-                wb_d = keep.tile([P, N], U32, name="wb_d", align_bytes=64)
+                wb_d = keep.tile([P, N], U32, name="wb_d", tag="reuse_w", align_bytes=64)
                 nc.vector.tensor_copy(
                     out=wb_d[:].rearrange("p (t c i) -> p c t i", t=PACK, i=4),
                     in_=wb_raw[:].rearrange("p (c i t) -> p c t i", t=PACK, i=4),
@@ -184,7 +186,7 @@ def tile_list_offsetpicks_timestable_residual_pl_kernel(
                 )
 
         y = [
-            keep.tile([P, PACK, HALF], F32, name="y%d" % h, tag=("reuse_hid", "y1")[h], align_bytes=64) for h in range(2)
+            keep.tile([P, PACK, HALF], F32, name="y%d" % h, tag=("reuse_u", "y1")[h], align_bytes=64) for h in range(2)
         ]
         y_bf = [keep.tile([P, HALF, PACK], BF16, name="y_bf%d" % h, align_bytes=64) for h in range(2)]
         y_codes = [keep.tile([P, HALF], U32, name="y_codes%d" % h, align_bytes=64) for h in range(2)]

@@ -152,7 +152,9 @@ def tile_list_offsetpicks_timestable_residual_pl_kernel(
 
         hid_codes = [keep.tile([P, HALF], U32, name="hid_codes%d" % h, align_bytes=64) for h in range(2)]
         hid_scales = [keep.tile([P, HALF], U8, name="hid_scales%d" % h, align_bytes=64) for h in range(2)]
-        p_ps = [psum.tile([P, PACK, HALF], F32, name="p_ps%d" % h) for h in range(2)]
+        p_first = [psum.tile([P, 2, HALF], F32, name="p_first%d" % i) for i in range(2)]
+        p_second = [psum.tile([P, HALF], F32, name="p_second%d" % t) for t in range(PACK)]
+        p_ps = [[p_first[t // 2][:, t % 2, :] for t in range(PACK)], [p_second[t][:] for t in range(PACK)]]
         for h in range(2):
             hid_bf = keep.tile([P, HALF, PACK], BF16, name="hid_bf%d" % h, align_bytes=64)
             nc.vector.scalar_tensor_tensor(
@@ -176,7 +178,7 @@ def tile_list_offsetpicks_timestable_residual_pl_kernel(
             )
             for t in range(PACK):
                 nc.tensor.matmul_mx(
-                    out=p_ps[h][:, t, :],
+                    out=p_ps[h][t],
                     lhsT=wb_d[:, P * t : P * (t + 1)].bitcast(E5M2),
                     lhsT_scale=wbs_d[:, P * t : P * (t + 1)],
                     rhs=hid_codes[h][:].bitcast(E5M2),
@@ -186,7 +188,7 @@ def tile_list_offsetpicks_timestable_residual_pl_kernel(
                 )
 
         y = [
-            keep.tile([P, PACK, HALF], F32, name="y%d" % h, tag=("reuse_u", "y1")[h], align_bytes=64) for h in range(2)
+            keep.tile([P, PACK, HALF], F32, name="y%d" % h, align_bytes=64) for h in range(2)
         ]
         y_bf = [keep.tile([P, HALF, PACK], BF16, name="y_bf%d" % h, align_bytes=64) for h in range(2)]
         y_codes = [keep.tile([P, HALF], U32, name="y_codes%d" % h, align_bytes=64) for h in range(2)]
@@ -195,7 +197,7 @@ def tile_list_offsetpicks_timestable_residual_pl_kernel(
             for t in range(PACK):
                 nc.vector.scalar_tensor_tensor(
                     out=y[h][:, t, :],
-                    in0=p_ps[h][:, t, :],
+                    in0=p_ps[h][t],
                     scalar=gm_sb[:, t : t + 1],
                     in1=rs_sb[:, t, HALVES[h]],
                     op0=ALU.mult,
@@ -203,18 +205,22 @@ def tile_list_offsetpicks_timestable_residual_pl_kernel(
                 )
             nc.sync.dma_start(out=by_slot(out_0)[:, :, HALVES[h]], in_=y[h][:])
         for h in range(2):
-            woven = y_bf[h][:].rearrange("p (c i) t -> p c t i", i=4)
-            source = y[h][:].rearrange("p t (c i) -> p c t i", i=4)
-            if h == 0:
-                nc.scalar.copy(out=woven, in_=source)
-            else:
-                nc.vector.tensor_copy(out=woven, in_=source)
+            on_scalar = (HALF, 80)[h]
+            nc.scalar.copy(
+                out=y_bf[h][:, :on_scalar, :].rearrange("p (c i) t -> p c t i", i=4),
+                in_=y[h][:, :, :on_scalar].rearrange("p t (c i) -> p c t i", i=4),
+            )
+            if h == 1:
+                nc.vector.tensor_copy(
+                    out=y_bf[h][:, on_scalar:, :].rearrange("p (c i) t -> p c t i", i=4),
+                    in_=y[h][:, :, on_scalar:].rearrange("p t (c i) -> p c t i", i=4),
+                )
             nc.vector.quantize_mx(
                 out=y_codes[h][:].bitcast(E4M3),
                 scales=y_scales[:, HALVES[h]],
                 in_=y_bf[h][:].rearrange("p j t -> p (j t)"),
             )
-            nc.scalar.dma_start(
+            (nc.sync, nc.scalar)[h].dma_start(
                 out=out_1[0, :, HALVES[h], :].rearrange("p j r -> p (j r)").bitcast(I32),
                 in_=y_codes[h][:].bitcast(I32),
             )

from contextlib import ExitStack

import concourse.mybir as mybir

K, T, J, R, V, N = 512, 1024, 256, 512, 512, 512
FLOPS = 2 * K * R * J + 2 * R * N * J

F32 = mybir.dt.float32
BF16 = mybir.dt.bfloat16
I32 = mybir.dt.int32
U32 = mybir.dt.uint32
U16 = mybir.dt.uint16
U8 = mybir.dt.uint8
E4M3 = mybir.dt.float8_e4m3fn_x4
E5M2 = mybir.dt.float8_e5m2_x4
E2M1 = mybir.dt.float4_e2m1fn_x4
ALU = mybir.AluOpType
COPY = mybir.ActivationFunctionType.Copy

P = 128
PACK = 4
HALF = J // 2
HALVES = (slice(0, HALF), slice(HALF, J))
LIST_HALVES = (slice(0, HALF // 16), slice(HALF // 16, J // 16))


def load_scale_rows(queue, plane, scales, quadrants):
    for q in quadrants:
        queue.dma_start(out=plane[32 * q : 32 * q + 4, :].bitcast(I32), in_=scales[0, 4 * q : 4 * q + 4, :].bitcast(I32))


def deal_scales(nc, dealt, plane):
    nc.vector.tensor_copy(
        out=dealt.rearrange("p (t c i) -> p c t i", t=PACK, i=16),
        in_=plane.rearrange("p (c i t) -> p c t i", t=PACK, i=16),
    )


def tile_list_offsetpicks_timestable_residual_pl_kernel(
    tc, xf, ow, fk, w_words, w_scales, tb, wb_words, wb_scales, rs, gm, offs, offs2, out_0, out_1, out_2
):
    nc = tc.nc
    with ExitStack() as ctx:
        keep = ctx.enter_context(tc.tile_pool(name="keep", bufs=1))
        psum = ctx.enter_context(tc.psum_pool(name="psum", bufs=1))

        def by_slot(x):
            return x.rearrange("(p t) c -> p t c", t=PACK)

        x_list = keep.tile([P, J // 16], U16, name="x_list")
        tb_list = keep.tile([P, J // 16], U16, name="tb_list")
        xf_sb = [keep.tile([P, T], F32, name="xf%d" % t) for t in range(PACK)]
        tb_pair = keep.tile([P, 2, V], F32, name="tb_pair")
        tb_rest = [keep.tile([P, V], F32, name="tb%d" % t) for t in range(2, PACK)]
        tb_sb = [tb_pair[:, 0, :], tb_pair[:, 1, :], tb_rest[0][:], tb_rest[1][:]]
        ow_sb = keep.tile([P, PACK, J], F32, name="ow_sb")
        rs_sb = keep.tile([P, PACK, J], F32, name="rs_sb")
        fk_sb = keep.tile([P, PACK], F32, name="fk_sb")
        gm_sb = keep.tile([P, PACK], F32, name="gm_sb")
        w_raw = keep.tile([P, 2 * R], U8, name="w_raw")
        wb_raw = keep.tile([P, N], U32, name="wb_raw")
        ws_raw = keep.tile([P, R], U8, name="ws_raw")
        wbs_raw = keep.tile([P, N], U8, name="wbs_raw")
        w_d = keep.tile([P, 2 * R], U8, name="w_d", tag="reuse_w", align_bytes=64)
        ws_d = keep.tile([P, R], U8, name="ws_d", align_bytes=64)

        nc.vector.memset(ws_raw[:].bitcast(I32), 0)
        nc.vector.memset(wbs_raw[:].bitcast(I32), 0)

        nc.sync.dma_start(out=xf_sb[0][:], in_=by_slot(xf)[:, 0, :])
        nc.sync.dma_start(x_list[:], offs)
        nc.sync.dma_start(out=fk_sb[:], in_=fk.rearrange("(p t) o -> p (t o)", t=PACK))
        nc.sync.dma_start(out=ow_sb[:], in_=by_slot(ow))
        load_scale_rows(nc.sync, ws_raw, w_scales, (0, 1, 2))
        nc.sync.dma_start(out=xf_sb[1][:], in_=by_slot(xf)[:, 1, :])
        load_scale_rows(nc.sync, ws_raw, w_scales, (3,))
        nc.sync.dma_start(out=w_raw[:].bitcast(I32), in_=w_words[0].bitcast(I32))
        nc.sync.dma_start(out=xf_sb[2][:], in_=by_slot(xf)[:, 2, :])
        nc.sync.dma_start(tb_list[:], offs2)
        load_scale_rows(nc.sync, wbs_raw, wb_scales, (0, 1))
        nc.sync.dma_start(out=xf_sb[3][:], in_=by_slot(xf)[:, 3, :])
        load_scale_rows(nc.sync, wbs_raw, wb_scales, (2, 3))
        nc.sync.dma_start(out=tb_pair[:], in_=by_slot(tb)[:, 0:2, :])
        for t in range(2, PACK):
            nc.sync.dma_start(out=tb_sb[t], in_=by_slot(tb)[:, t, :])
        nc.sync.dma_start(
            out=wb_raw[:].bitcast(I32), in_=wb_words[0].rearrange("p c r -> p (c r)").bitcast(I32)
        )
        nc.sync.dma_start(out=gm_sb[:], in_=gm.rearrange("(p t) o -> p (t o)", t=PACK))
        nc.sync.dma_start(out=rs_sb[:], in_=by_slot(rs))


        diff_pair = [keep.tile([P, 2, J], F32, name="diff%d" % i, tag="reuse%d" % i, align_bytes=64) for i in range(2)]
        diff = [diff_pair[t // 2][:, t % 2, :] for t in range(PACK)]
        u_bf = keep.tile([P, J, PACK], BF16, name="u_bf", tag="reuse_u", align_bytes=64)
        u_codes = keep.tile([P, J], U32, name="u_codes", align_bytes=64)
        u_scales = keep.tile([P, J], U8, name="u_scales", align_bytes=64)
        last = PACK - 1
        for t in range(last):
            nc.vector.tensor_tensor(diff[t], xf_sb[t][:].indirect(x_list[:]), ow_sb[:, t, :], ALU.subtract)
            nc.scalar.activation(out=u_bf[:, :, t], in_=diff[t], func=COPY, scale=fk_sb[:, t : t + 1])
            if t == 1:
                nc.vector.tensor_copy(
                    out=w_d[:].bitcast(U16).rearrange("p (t c i) -> p c t i", t=PACK, i=8),
                    in_=w_raw[:].bitcast(U16).rearrange("p (c i t) -> p c t i", t=PACK, i=8),
                )
                deal_scales(nc, ws_d[:], ws_raw[:])
        for h in range(2):
            nc.vector.tensor_tensor(
                diff[last][:, HALVES[h]],
                xf_sb[last][:].indirect(x_list[:, LIST_HALVES[h]]),
                ow_sb[:, last, HALVES[h]],
                ALU.subtract,
            )
            nc.scalar.activation(
                out=u_bf[:, HALVES[h], last],
                in_=diff[last][:, HALVES[h]],
                func=COPY,
                scale=fk_sb[:, last : last + 1],
            )
        wbs_d = keep.tile([P, N], U8, name="wbs_d", align_bytes=64)
        deal_scales(nc, wbs_d[:], wbs_raw[:])
        a_ps = [psum.tile([P, PACK, HALF], F32, name="a_ps%d" % h) for h in range(2)]
        for h in range(2):
            nc.vector.quantize_mx(
                out=u_codes[:, HALVES[h]].bitcast(E4M3),
                scales=u_scales[:, HALVES[h]],
                in_=u_bf[:, HALVES[h], :].rearrange("p j t -> p (j t)"),
            )
            for t in range(PACK):
                nc.tensor.matmul_mx(
                    out=a_ps[h][:, t, :],
                    lhsT=w_d[:, 2 * P * t : 2 * P * (t + 1)].bitcast(E2M1),
                    lhsT_scale=ws_d[:, P * t : P * (t + 1)],
                    rhs=u_codes[:, HALVES[h]].bitcast(E4M3),
                    rhs_scale=u_scales[:, HALVES[h]],
                    start=True,
                    stop=True,
                )

        tb_g = [
            keep.tile([P, PACK, HALF], F32, name="tb_g%d" % h, tag=("reuse1", "reuse_u")[h], align_bytes=64)
            for h in range(2)
        ]
        for h in range(2):
            for t in range(PACK):
                picked = tb_sb[t].indirect(tb_list[:, LIST_HALVES[h]])
                if h == 0 and t >= 2:
                    nc.vector.tensor_copy(out=tb_g[h][:, t, :], in_=picked)
                else:
                    nc.scalar.activation(out=tb_g[h][:, t, :], in_=picked, func=COPY)

        hid_codes = [keep.tile([P, HALF], U32, name="hid_codes%d" % h, align_bytes=64) for h in range(2)]
        hid_scales = [keep.tile([P, HALF], U8, name="hid_scales%d" % h, align_bytes=64) for h in range(2)]
        p_first = [psum.tile([P, 2, HALF], F32, name="p_first%d" % i) for i in range(2)]
        p_second = [psum.tile([P, HALF], F32, name="p_second%d" % t) for t in range(PACK)]
        p_ps = [[p_first[t // 2][:, t % 2, :] for t in range(PACK)], [p_second[t][:] for t in range(PACK)]]
        for h in range(2):
            hid_bf = keep.tile([P, HALF, PACK], BF16, name="hid_bf%d" % h, align_bytes=64)
            nc.vector.scalar_tensor_tensor(
                out=hid_bf[:],
                in0=a_ps[h][:].rearrange("p t j -> p j t"),
                scalar=0.0,
                in1=tb_g[h][:].rearrange("p t j -> p j t"),
                op0=ALU.max,
                op1=ALU.mult,
            )
            if h == 0:
                wb_d = keep.tile([P, N], U32, name="wb_d", tag="reuse_w", align_bytes=64)
                nc.vector.tensor_copy(
                    out=wb_d[:].rearrange("p (t c i) -> p c t i", t=PACK, i=4),
                    in_=wb_raw[:].rearrange("p (c i t) -> p c t i", t=PACK, i=4),
                )
            nc.vector.quantize_mx(
                out=hid_codes[h][:].bitcast(E5M2),
                scales=hid_scales[h][:],
                in_=hid_bf[:].rearrange("p j t -> p (j t)"),
            )
            for t in range(PACK):
                nc.tensor.matmul_mx(
                    out=p_ps[h][t],
                    lhsT=wb_d[:, P * t : P * (t + 1)].bitcast(E5M2),
                    lhsT_scale=wbs_d[:, P * t : P * (t + 1)],
                    rhs=hid_codes[h][:].bitcast(E5M2),
                    rhs_scale=hid_scales[h][:],
                    start=True,
                    stop=True,
                )

        y = [
            keep.tile([P, PACK, HALF], F32, name="y%d" % h, align_bytes=64) for h in range(2)
        ]
        y_bf = [keep.tile([P, HALF, PACK], BF16, name="y_bf%d" % h, align_bytes=64) for h in range(2)]
        y_codes = [keep.tile([P, HALF], U32, name="y_codes%d" % h, align_bytes=64) for h in range(2)]
        y_scales = keep.tile([P, J], U8, name="y_scales", align_bytes=64)
        for h in range(2):
            for t in range(PACK):
                nc.vector.scalar_tensor_tensor(
                    out=y[h][:, t, :],
                    in0=p_ps[h][t],
                    scalar=gm_sb[:, t : t + 1],
                    in1=rs_sb[:, t, HALVES[h]],
                    op0=ALU.mult,
                    op1=ALU.add,
                )
            nc.sync.dma_start(out=by_slot(out_0)[:, :, HALVES[h]], in_=y[h][:])
        for h in range(2):
            on_scalar = (HALF, 80)[h]
            nc.scalar.copy(
                out=y_bf[h][:, :on_scalar, :].rearrange("p (c i) t -> p c t i", i=4),
                in_=y[h][:, :, :on_scalar].rearrange("p t (c i) -> p c t i", i=4),
            )
            if h == 1:
                nc.vector.tensor_copy(
                    out=y_bf[h][:, on_scalar:, :].rearrange("p (c i) t -> p c t i", i=4),
                    in_=y[h][:, :, on_scalar:].rearrange("p t (c i) -> p c t i", i=4),
                )
            nc.vector.quantize_mx(
                out=y_codes[h][:].bitcast(E4M3),
                scales=y_scales[:, HALVES[h]],
                in_=y_bf[h][:].rearrange("p j t -> p (j t)"),
            )
            (nc.sync, nc.scalar)[h].dma_start(
                out=out_1[0, :, HALVES[h], :].rearrange("p j r -> p (j r)").bitcast(I32),
                in_=y_codes[h][:].bitcast(I32),
            )
        for q in range(4):
            queue = nc.sync if q % 2 == 0 else nc.scalar
            queue.dma_start(
                out=out_2[0, 4 * q : 4 * q + 4, :].bitcast(I32), in_=y_scales[32 * q : 32 * q + 4, :].bitcast(I32)
            )
